import numpy as np
import ml_dtypes


def mxq(x, axis, fmt="e4m3"):
    dtype, down = {"e4m3": (ml_dtypes.float8_e4m3fn, 7), "e5m2": (ml_dtypes.float8_e5m2, 14)}[fmt]
    v = np.moveaxis(np.asarray(x, np.float32).astype(ml_dtypes.bfloat16).astype(np.float64), axis, -1)
    blocks = v.reshape(v.shape[:-1] + (-1, 32))
    amax = np.abs(blocks).max(-1, keepdims=True)
    byte = np.maximum(np.where(amax > 0, np.frexp(amax)[1] - 1 + 127, 0) - down, 1)
    scale = np.exp2(byte - 127.0)
    codes = (blocks / scale).astype(np.float32).astype(dtype).astype(np.float64)
    return np.moveaxis((codes * scale).reshape(v.shape), -1, axis)


WIDE = False


def mx_kscale(k):
    if not WIDE:
        return np.ones(k)
    levels = np.array([30, -30])
    if k % 512:
        return np.exp2(np.random.permutation(np.resize(levels, k // 32))).repeat(32)
    a = np.empty((k // 512, 16))
    for p in range(k // 512):
        a[p, :8] = np.random.permutation(np.resize(levels, 8))
        for g in range(8):
            far = levels[np.abs(levels - a[p, g]) >= 10]
            a[p, g + 8] = far[np.random.randint(len(far))]
    return np.exp2(a.ravel()).repeat(32)


def f64(x):
    return np.asarray(x).astype(np.float64)


def striped(idx):
    return np.tile(np.asarray(idx).reshape(-1, 16).T, (8, 1)).astype(np.uint16)


def unstriped(offs):
    return offs[:16].T.reshape(-1).astype(np.int64)


E2M1 = np.array([0.0, 0.5, 1.0, 1.5, 2.0, 3.0, 4.0, 6.0, -0.0, -0.5, -1.0, -1.5, -2.0, -3.0, -4.0, -6.0])


def pack_weight(w, fmt):
    k, n = w.shape
    w = f64(np.asarray(w, np.float32).astype(ml_dtypes.bfloat16)).reshape(k // 32, 32, n)
    amax = np.abs(w).max(1)
    if fmt == "e4m3":
        byte = np.frexp(amax)[1] - 1 + 127 - 7
    else:
        mant, ex = np.frexp(amax / 6.0)
        byte = np.where(mant > 0.5, ex, ex - 1) + 127
    byte = np.clip(np.where(amax > 0, byte, 1), 1, 254)
    scaled = (w * np.exp2(127.0 - byte)[:, None, :]).reshape(k, n).astype(np.float32)
    by_word = np.ascontiguousarray(scaled.reshape(k // 512, 128, 4, n).transpose(0, 1, 3, 2))
    if fmt == "e4m3":
        words = by_word.astype(ml_dtypes.float8_e4m3fn).view(np.uint8)
    else:
        c = by_word.astype(ml_dtypes.float4_e2m1fn).view(np.uint8) & 0xF
        words = (c[..., 0::2] | (c[..., 1::2] << 4)).reshape(k // 512, 128, 2 * n)
    return np.ascontiguousarray(words), np.ascontiguousarray(byte.astype(np.uint8).reshape(k // 512, 16, n))


def unpack_weight(words, scales, fmt):
    g, _, n = scales.shape
    words = np.ascontiguousarray(words).reshape(g, 128, n, -1)
    if fmt == "e4m3":
        vals = words.view(ml_dtypes.float8_e4m3fn).astype(np.float64)
    else:
        nib = np.empty((g, 128, n, 4), np.uint8)
        nib[..., 0::2] = words & 0xF
        nib[..., 1::2] = words >> 4
        vals = E2M1[nib]
    vals = vals * np.repeat(np.exp2(scales.astype(np.float64) - 127.0), 8, axis=1)[..., None]
    return vals.transpose(0, 1, 3, 2).reshape(g * 512, n)


def bf(x):
    return np.asarray(x, np.float32).astype(ml_dtypes.bfloat16)


def planes(Y):
    r, m = Y.shape
    b = f64(bf(Y)).reshape(r // 32, 32, m)
    amax = np.abs(b).max(1)
    byte = np.clip(np.where(amax > 0, np.frexp(amax)[1] - 1 + 127 - 7, 1), 1, 254)
    codes = (b * np.exp2(127.0 - byte)[:, None, :]).reshape(r, m).astype(np.float32).astype(ml_dtypes.float8_e4m3fn).view(np.uint8)
    words = codes.reshape(r // 512, 128, 4, m).transpose(0, 1, 3, 2)
    return np.ascontiguousarray(words), np.ascontiguousarray(byte.astype(np.uint8).reshape(r // 512, 16, m))


K, N, T, J = 512, 1024, 2048, 512


def setup_inputs():
    n = np.random.standard_normal
    idx = np.random.permutation(T)[:J]
    fn = mx_kscale(N)
    wp = pack_weight(n((N, K)) * 1 / np.sqrt(N) * fn[:, None], "e4m3")
    return {
        "g": (n((N, T)) * np.exp(0.5 * n((1, T))) / fn[:, None]).astype(np.float32),
        "w_words": wp[0],
        "w_scales": wp[1],
        "xh": (n((K, T))).astype(np.float32),
        "inv": (np.random.uniform(0.5, 2.0, (J, 1))).astype(np.float32),
        "offs": striped(idx),
    }


def reference(g, w_words, w_scales, xh, inv, offs):
    idx = unstriped(offs)
    wu = unpack_weight(w_words, w_scales, "e4m3")
    gidxq = mxq(f64(g)[:, idx], 0, "e5m2")
    gq = gidxq.T @ wu
    xj = f64(xh)[:, idx].T
    y = f64(inv) * (gq - xj * np.mean(gq * xj, axis=1, keepdims=True))
    words, scales = planes(y)
    return y, words, scales

@@ -1,0 +1,161 @@
+from contextlib import ExitStack
+
+import concourse.mybir as mybir
+from concourse.masks import make_identity
+
+K, N, T, J = 512, 1024, 2048, 512
+FLOPS = 2 * J * N * K
+
+F32 = mybir.dt.float32
+BF16 = mybir.dt.bfloat16
+I32 = mybir.dt.int32
+U32 = mybir.dt.uint32
+U16 = mybir.dt.uint16
+U8 = mybir.dt.uint8
+E4M3 = mybir.dt.float8_e4m3fn_x4
+E5M2 = mybir.dt.float8_e5m2_x4
+MULT = mybir.AluOpType.mult
+ADD = mybir.AluOpType.add
+COPY = mybir.ActivationFunctionType.Copy
+IDENTITY = mybir.ActivationFunctionType.Identity
+
+P = 128
+PACK = 4
+PASSES = N // (P * PACK)
+BLOCKS = K // P
+HALF = K // 2
+
+
+def tile_list_unit_size_back_pl_kernel(tc, g, w_words, w_scales, xh, inv, offs, out_0, out_1, out_2):
+    nc = tc.nc
+    with ExitStack() as ctx:
+        keep = ctx.enter_context(tc.tile_pool(name="keep", bufs=1))
+        psum = ctx.enter_context(tc.psum_pool(name="psum", bufs=1))
+
+        offsets = keep.tile([P, J // 16], U16, name="offsets")
+        g_rows = [keep.tile([P, T], F32, name="g_rows%d" % n) for n in range(PASSES * PACK)]
+        x_rows = [keep.tile([P, T], F32, name="x_rows%d" % b) for b in range(BLOCKS)]
+        w_codes = keep.tile([P, PASSES, K], U32, name="w_codes", align_bytes=64)
+        w_plane = keep.tile([P, PASSES, K], U8, name="w_plane", align_bytes=64)
+        inv_col = keep.tile([P, PACK], F32, name="inv_col")
+        ident = keep.tile([P, P], F32, name="ident")
+
+        g_view = g.rearrange("(a p i) t -> a i p t", a=PASSES, i=PACK)
+        for n in range(PASSES * PACK):
+            nc.sync.dma_start(out=g_rows[n][:], in_=g_view[n // PACK, n % PACK])
+            if n == 0:
+                nc.sync.dma_start(offsets[:], offs)
+        nc.sync.dma_start(
+            out=w_codes[:].bitcast(I32),
+            in_=w_words.rearrange("z p c r -> p z (c r)").bitcast(I32),
+        )
+        for b in range(BLOCKS):
+            nc.sync.dma_start(out=x_rows[b][:], in_=xh[b * P : (b + 1) * P, :])
+
+        nc.gpsimd.memset(w_plane[:].bitcast(I32), 0)
+        for q in range(4):
+            nc.gpsimd.dma_start(
+                out=w_plane[32 * q : 32 * q + 4, :, :].bitcast(I32),
+                in_=w_scales[:, 4 * q : 4 * q + 4, :].rearrange("z r c -> r z c").bitcast(I32),
+            )
+        nc.gpsimd.dma_start(out=inv_col[:], in_=inv.rearrange("(p t) o -> p (t o)", t=PACK))
+        make_identity(nc, ident[:])
+
+        acc = [psum.tile([P, K], F32, name="acc%d" % t) for t in range(PACK)]
+        xj = [psum.tile([P, K], F32, name="xj%d" % t) for t in range(PACK)]
+        scaled = [keep.tile([P, K], F32, name="scaled%d" % t) for t in range(PACK)]
+
+        for a in range(PASSES):
+            picked = keep.tile([P, PACK, J], BF16, name="picked%d" % a)
+            for i in range(PACK):
+                nc.vector.tensor_copy(out=picked[:, i, :], in_=g_rows[PACK * a + i][:].indirect(offsets[:]))
+            grouped = keep.tile([P, PACK, P, PACK], BF16, name="grouped%d" % a, align_bytes=64)
+            dealt = picked[:].rearrange("p i (m t) -> p t m i", t=PACK)
+            if a == 0:
+                nc.scalar.copy(out=grouped[:], in_=dealt)
+            else:
+                nc.vector.tensor_copy(out=grouped[:], in_=dealt)
+            g_codes = keep.tile([P, J], U32, name="g_codes%d" % a, align_bytes=64)
+            g_plane = keep.tile([P, J], U8, name="g_plane%d" % a, align_bytes=64)
+            nc.vector.quantize_mx(
+                out=g_codes[:].bitcast(E5M2),
+                scales=g_plane[:],
+                in_=grouped[:].rearrange("p t m i -> p (t m i)"),
+            )
+            for t in range(PACK):
+                cols = slice(P * t, P * (t + 1))
+                nc.tensor.matmul_mx(
+                    out=acc[t][:],
+                    lhsT=g_codes[:, cols].bitcast(E5M2),
+                    lhsT_scale=g_plane[:, cols],
+                    rhs=w_codes[:, a, :].bitcast(E4M3),
+                    rhs_scale=w_plane[:, a, :],
+                    start=(a == 0),
+                    stop=(a == PASSES - 1),
+                )
+        for t in range(PACK):
+            nc.scalar.activation(out=scaled[t][:], in_=acc[t][:], func=COPY, scale=inv_col[:, t : t + 1])
+
+        product = keep.tile([P, HALF], F32, name="product")
+        parts = [keep.tile([P, PACK], F32, name="parts%d" % h) for h in range(2)]
+        coef = keep.tile([P, PACK], F32, name="coef")
+        for h in range(2):
+            for b in range(2 * h, 2 * h + 2):
+                x_picked = keep.tile([P, J], F32, name="x_picked%d" % b)
+                nc.vector.tensor_copy(out=x_picked[:], in_=x_rows[b][:].indirect(offsets[:]))
+                for t in range(PACK):
+                    nc.tensor.transpose(xj[t][:, b * P : (b + 1) * P], x_picked[:, t::PACK], ident[:])
+            cols = slice(h * HALF, (h + 1) * HALF)
+            for t in range(PACK):
+                nc.vector.scalar_tensor_tensor(
+                    out=product[:],
+                    in0=xj[t][:, cols],
+                    scalar=-1.0 / K,
+                    in1=scaled[t][:, cols],
+                    op0=MULT,
+                    op1=MULT,
+                    accum_out=parts[h][:, t : t + 1],
+                )
+        for t in range(PACK):
+            nc.scalar.activation(
+                out=coef[:, t : t + 1], in_=parts[1][:, t : t + 1], func=IDENTITY, bias=parts[0][:, t : t + 1]
+            )
+
+        y_codes = keep.tile([P, K], U32, name="y_codes", align_bytes=64)
+        y_plane = keep.tile([P, K], U8, name="y_plane", align_bytes=64)
+        out_rows = out_0.rearrange("(p t) k -> p t k", t=PACK)
+        out_words = out_1[0].rearrange("p c r -> p (c r)").bitcast(I32)
+        rounded = []
+        for h in range(2):
+            cols = slice(h * HALF, (h + 1) * HALF)
+            y = keep.tile([P, PACK, HALF], F32, name="y%d" % h)
+            for t in range(PACK):
+                nc.vector.scalar_tensor_tensor(
+                    out=y[:, t, :],
+                    in0=xj[t][:, cols],
+                    scalar=coef[:, t : t + 1],
+                    in1=scaled[t][:, cols],
+                    op0=MULT,
+                    op1=ADD,
+                )
+            nc.sync.dma_start(out=out_rows[:, :, cols], in_=y[:])
+            y_bf = keep.tile([P, HALF, PACK], BF16, name="y_bf%d" % h, align_bytes=64)
+            if h == 0:
+                nc.scalar.copy(out=y_bf[:], in_=y[:].rearrange("p t k -> p k t"))
+            else:
+                nc.vector.tensor_copy(out=y_bf[:], in_=y[:].rearrange("p t k -> p k t"))
+            rounded.append(y_bf)
+        for h in range(2):
+            cols = slice(h * HALF, (h + 1) * HALF)
+            nc.vector.quantize_mx(
+                out=y_codes[:, cols].bitcast(E4M3),
+                scales=y_plane[:, cols],
+                in_=rounded[h][:].rearrange("p k t -> p (k t)"),
+            )
+            nc.sync.dma_start(out=out_words[:, cols], in_=y_codes[:, cols].bitcast(I32))
+        for q in range(4):
+            queue = nc.scalar if q < 2 else nc.sync
+            queue.dma_start(
+                out=out_2[0, 4 * q : 4 * q + 4, :].bitcast(I32),
+                in_=y_plane[32 * q : 32 * q + 4, :].bitcast(I32),
+            )

@@ -17,13 +17,14 @@ E5M2 = mybir.dt.float8_e5m2_x4
 MULT = mybir.AluOpType.mult
 ADD = mybir.AluOpType.add
 COPY = mybir.ActivationFunctionType.Copy
-IDENTITY = mybir.ActivationFunctionType.Identity
 
 P = 128
 PACK = 4
 PASSES = N // (P * PACK)
 BLOCKS = K // P
 HALF = K // 2
+BLOCK_ORDER = (0, 2, 1, 3)
+SCALAR_RUNS = 28
 
 
 def tile_list_unit_size_back_pl_kernel(tc, g, w_words, w_scales, xh, inv, offs, out_0, out_1, out_2):
@@ -34,47 +35,53 @@ def tile_list_unit_size_back_pl_kernel(tc, g, w_words, w_scales, xh, inv, offs, 
 
         offsets = keep.tile([P, J // 16], U16, name="offsets")
         g_rows = [keep.tile([P, T], F32, name="g_rows%d" % n) for n in range(PASSES * PACK)]
-        x_rows = [keep.tile([P, T], F32, name="x_rows%d" % b) for b in range(BLOCKS)]
+        x_rows = [keep.tile([P, T], F32, name="x_rows%d" % b, tag="x_rows%d" % b) for b in range(BLOCKS)]
         w_codes = keep.tile([P, PASSES, K], U32, name="w_codes", align_bytes=64)
         w_plane = keep.tile([P, PASSES, K], U8, name="w_plane", align_bytes=64)
         inv_col = keep.tile([P, PACK], F32, name="inv_col")
         ident = keep.tile([P, P], F32, name="ident")
 
+        make_identity(nc, ident[:])
+        nc.vector.memset(w_plane[:].bitcast(I32), 0)
         g_view = g.rearrange("(a p i) t -> a i p t", a=PASSES, i=PACK)
         for n in range(PASSES * PACK):
             nc.sync.dma_start(out=g_rows[n][:], in_=g_view[n // PACK, n % PACK])
             if n == 0:
                 nc.sync.dma_start(offsets[:], offs)
+            if n == 2:
+                for q in range(4):
+                    nc.sync.dma_start(
+                        out=w_plane[32 * q : 32 * q + 4, :, :].bitcast(I32),
+                        in_=w_scales[:, 4 * q : 4 * q + 4, :].rearrange("z r c -> r z c").bitcast(I32),
+                    )
+                nc.sync.dma_start(out=inv_col[:], in_=inv.rearrange("(p t) o -> p (t o)", t=PACK))
         nc.sync.dma_start(
             out=w_codes[:].bitcast(I32),
             in_=w_words.rearrange("z p c r -> p z (c r)").bitcast(I32),
         )
-        for b in range(BLOCKS):
+        for b in BLOCK_ORDER:
             nc.sync.dma_start(out=x_rows[b][:], in_=xh[b * P : (b + 1) * P, :])
 
-        nc.gpsimd.memset(w_plane[:].bitcast(I32), 0)
-        for q in range(4):
-            nc.gpsimd.dma_start(
-                out=w_plane[32 * q : 32 * q + 4, :, :].bitcast(I32),
-                in_=w_scales[:, 4 * q : 4 * q + 4, :].rearrange("z r c -> r z c").bitcast(I32),
-            )
-        nc.gpsimd.dma_start(out=inv_col[:], in_=inv.rearrange("(p t) o -> p (t o)", t=PACK))
-        make_identity(nc, ident[:])
 
         acc = [psum.tile([P, K], F32, name="acc%d" % t) for t in range(PACK)]
-        xj = [psum.tile([P, K], F32, name="xj%d" % t) for t in range(PACK)]
+        low = [psum.tile([P, K], F32, name="low%d" % t) for t in range(PACK)]
+        xj = [[low[t][:, :HALF] for t in range(PACK)], [acc[t][:, :HALF] for t in range(PACK)]]
         scaled = [keep.tile([P, K], F32, name="scaled%d" % t) for t in range(PACK)]
 
         for a in range(PASSES):
             picked = keep.tile([P, PACK, J], BF16, name="picked%d" % a)
             for i in range(PACK):
-                nc.vector.tensor_copy(out=picked[:, i, :], in_=g_rows[PACK * a + i][:].indirect(offsets[:]))
+                nc.vector.tensor_copy(
+                    out=picked[:, i, :],
+                    in_=g_rows[PACK * a + i][:].indirect(offsets[:]),
+                )
             grouped = keep.tile([P, PACK, P, PACK], BF16, name="grouped%d" % a, align_bytes=64)
-            dealt = picked[:].rearrange("p i (m t) -> p t m i", t=PACK)
+            source = picked[:].rearrange("p i (m t) -> p m i t", t=PACK)
+            dealt = grouped[:].rearrange("p t m i -> p m i t")
             if a == 0:
-                nc.scalar.copy(out=grouped[:], in_=dealt)
+                nc.scalar.copy(out=dealt, in_=source)
             else:
-                nc.vector.tensor_copy(out=grouped[:], in_=dealt)
+                nc.vector.tensor_copy(out=dealt, in_=source)
             g_codes = keep.tile([P, J], U32, name="g_codes%d" % a, align_bytes=64)
             g_plane = keep.tile([P, J], U8, name="g_plane%d" % a, align_bytes=64)
             nc.vector.quantize_mx(
@@ -96,30 +103,35 @@ def tile_list_unit_size_back_pl_kernel(tc, g, w_words, w_scales, xh, inv, offs, 
         for t in range(PACK):
             nc.scalar.activation(out=scaled[t][:], in_=acc[t][:], func=COPY, scale=inv_col[:, t : t + 1])
 
-        product = keep.tile([P, HALF], F32, name="product")
-        parts = [keep.tile([P, PACK], F32, name="parts%d" % h) for h in range(2)]
+        parts = keep.tile([P, PACK, BLOCKS], F32, name="parts")
         coef = keep.tile([P, PACK], F32, name="coef")
-        for h in range(2):
-            for b in range(2 * h, 2 * h + 2):
-                x_picked = keep.tile([P, J], F32, name="x_picked%d" % b)
-                nc.vector.tensor_copy(out=x_picked[:], in_=x_rows[b][:].indirect(offsets[:]))
-                for t in range(PACK):
-                    nc.tensor.transpose(xj[t][:, b * P : (b + 1) * P], x_picked[:, t::PACK], ident[:])
-            cols = slice(h * HALF, (h + 1) * HALF)
+        spare = keep.tile([P, PACK, BLOCKS], F32, name="spare")
+
+        def partial_sums(b, tag):
+            product = keep.tile([P, PACK, P], F32, name="product%d" % b, tag=tag)
             for t in range(PACK):
                 nc.vector.scalar_tensor_tensor(
-                    out=product[:],
-                    in0=xj[t][:, cols],
+                    out=product[:, t, :],
+                    in0=xj[b // 2][t][:, (b % 2) * P : (b % 2 + 1) * P],
                     scalar=-1.0 / K,
-                    in1=scaled[t][:, cols],
+                    in1=scaled[t][:, b * P : (b + 1) * P],
                     op0=MULT,
                     op1=MULT,
-                    accum_out=parts[h][:, t : t + 1],
+                    accum_out=parts[:, t, b : b + 1],
                 )
+
+        for n, b in enumerate(BLOCK_ORDER):
+            x_picked = keep.tile([P, J], F32, name="x_picked%d" % b)
+            nc.vector.tensor_copy(out=x_picked[:], in_=x_rows[b][:].indirect(offsets[:]))
+            for t in range(PACK):
+                nc.tensor.transpose(
+                    xj[b // 2][t][:, (b % 2) * P : (b % 2 + 1) * P], x_picked[:, t::PACK], ident[:]
+                )
+            if n > 0:
+                partial_sums(BLOCK_ORDER[n - 1], "x_rows%d" % b)
+        partial_sums(BLOCK_ORDER[-1], "last_product")
         for t in range(PACK):
-            nc.scalar.activation(
-                out=coef[:, t : t + 1], in_=parts[1][:, t : t + 1], func=IDENTITY, bias=parts[0][:, t : t + 1]
-            )
+            nc.scalar.activation(out=spare[:, t, :], in_=parts[:, t, :], func=COPY, accum_out=coef[:, t : t + 1])
 
         y_codes = keep.tile([P, K], U32, name="y_codes", align_bytes=64)
         y_plane = keep.tile([P, K], U8, name="y_plane", align_bytes=64)
@@ -132,18 +144,22 @@ def tile_list_unit_size_back_pl_kernel(tc, g, w_words, w_scales, xh, inv, offs, 
             for t in range(PACK):
                 nc.vector.scalar_tensor_tensor(
                     out=y[:, t, :],
-                    in0=xj[t][:, cols],
+                    in0=xj[h][t],
                     scalar=coef[:, t : t + 1],
                     in1=scaled[t][:, cols],
                     op0=MULT,
                     op1=ADD,
                 )
-            nc.sync.dma_start(out=out_rows[:, :, cols], in_=y[:])
+                if t % 2 == 1:
+                    nc.sync.dma_start(out=out_rows[:, t - 1 : t + 1, cols], in_=y[:, t - 1 : t + 1, :])
             y_bf = keep.tile([P, HALF, PACK], BF16, name="y_bf%d" % h, align_bytes=64)
+            source = y[:].rearrange("p t (c i) -> p c t i", i=PACK)
+            woven = y_bf[:].rearrange("p (c i) t -> p c t i", i=PACK)
             if h == 0:
-                nc.scalar.copy(out=y_bf[:], in_=y[:].rearrange("p t k -> p k t"))
+                nc.scalar.copy(out=woven, in_=source)
             else:
-                nc.vector.tensor_copy(out=y_bf[:], in_=y[:].rearrange("p t k -> p k t"))
+                nc.scalar.copy(out=woven[:, :SCALAR_RUNS], in_=source[:, :SCALAR_RUNS])
+                nc.vector.tensor_copy(out=woven[:, SCALAR_RUNS:], in_=source[:, SCALAR_RUNS:])
             rounded.append(y_bf)
         for h in range(2):
             cols = slice(h * HALF, (h + 1) * HALF)

@@ -150,8 +150,8 @@ def tile_list_unit_size_back_pl_kernel(tc, g, w_words, w_scales, xh, inv, offs, 
                     op0=MULT,
                     op1=ADD,
                 )
-                if t % 2 == 1:
-                    nc.sync.dma_start(out=out_rows[:, t - 1 : t + 1, cols], in_=y[:, t - 1 : t + 1, :])
+                if (t + 1) % (h + 1) == 0:
+                    nc.sync.dma_start(out=out_rows[:, t - h : t + 1, cols], in_=y[:, t - h : t + 1, :])
             y_bf = keep.tile([P, HALF, PACK], BF16, name="y_bf%d" % h, align_bytes=64)
             source = y[:].rearrange("p t (c i) -> p c t i", i=PACK)
             woven = y_bf[:].rearrange("p (c i) t -> p c t i", i=PACK)

from contextlib import ExitStack

import concourse.mybir as mybir
from concourse.masks import make_identity

K, N, T, J = 512, 1024, 2048, 512
FLOPS = 2 * J * N * K

F32 = mybir.dt.float32
BF16 = mybir.dt.bfloat16
I32 = mybir.dt.int32
U32 = mybir.dt.uint32
U16 = mybir.dt.uint16
U8 = mybir.dt.uint8
E4M3 = mybir.dt.float8_e4m3fn_x4
E5M2 = mybir.dt.float8_e5m2_x4
MULT = mybir.AluOpType.mult
ADD = mybir.AluOpType.add
COPY = mybir.ActivationFunctionType.Copy

P = 128
PACK = 4
PASSES = N // (P * PACK)
BLOCKS = K // P
HALF = K // 2
BLOCK_ORDER = (0, 2, 1, 3)
SCALAR_RUNS = 28


def tile_list_unit_size_back_pl_kernel(tc, g, w_words, w_scales, xh, inv, offs, out_0, out_1, out_2):
    nc = tc.nc
    with ExitStack() as ctx:
        keep = ctx.enter_context(tc.tile_pool(name="keep", bufs=1))
        psum = ctx.enter_context(tc.psum_pool(name="psum", bufs=1))

        offsets = keep.tile([P, J // 16], U16, name="offsets")
        g_rows = [keep.tile([P, T], F32, name="g_rows%d" % n) for n in range(PASSES * PACK)]
        x_rows = [keep.tile([P, T], F32, name="x_rows%d" % b, tag="x_rows%d" % b) for b in range(BLOCKS)]
        w_codes = keep.tile([P, PASSES, K], U32, name="w_codes", align_bytes=64)
        w_plane = keep.tile([P, PASSES, K], U8, name="w_plane", align_bytes=64)
        inv_col = keep.tile([P, PACK], F32, name="inv_col")
        ident = keep.tile([P, P], F32, name="ident")

        make_identity(nc, ident[:])
        nc.vector.memset(w_plane[:].bitcast(I32), 0)
        g_view = g.rearrange("(a p i) t -> a i p t", a=PASSES, i=PACK)
        for n in range(PASSES * PACK):
            nc.sync.dma_start(out=g_rows[n][:], in_=g_view[n // PACK, n % PACK])
            if n == 0:
                nc.sync.dma_start(offsets[:], offs)
            if n == 2:
                for q in range(4):
                    nc.sync.dma_start(
                        out=w_plane[32 * q : 32 * q + 4, :, :].bitcast(I32),
                        in_=w_scales[:, 4 * q : 4 * q + 4, :].rearrange("z r c -> r z c").bitcast(I32),
                    )
                nc.sync.dma_start(out=inv_col[:], in_=inv.rearrange("(p t) o -> p (t o)", t=PACK))
        nc.sync.dma_start(
            out=w_codes[:].bitcast(I32),
            in_=w_words.rearrange("z p c r -> p z (c r)").bitcast(I32),
        )
        for b in BLOCK_ORDER:
            nc.sync.dma_start(out=x_rows[b][:], in_=xh[b * P : (b + 1) * P, :])


        acc = [psum.tile([P, K], F32, name="acc%d" % t) for t in range(PACK)]
        low = [psum.tile([P, K], F32, name="low%d" % t) for t in range(PACK)]
        xj = [[low[t][:, :HALF] for t in range(PACK)], [acc[t][:, :HALF] for t in range(PACK)]]
        scaled = [keep.tile([P, K], F32, name="scaled%d" % t) for t in range(PACK)]

        for a in range(PASSES):
            picked = keep.tile([P, PACK, J], BF16, name="picked%d" % a)
            for i in range(PACK):
                nc.vector.tensor_copy(
                    out=picked[:, i, :],
                    in_=g_rows[PACK * a + i][:].indirect(offsets[:]),
                )
            grouped = keep.tile([P, PACK, P, PACK], BF16, name="grouped%d" % a, align_bytes=64)
            source = picked[:].rearrange("p i (m t) -> p m i t", t=PACK)
            dealt = grouped[:].rearrange("p t m i -> p m i t")
            if a == 0:
                nc.scalar.copy(out=dealt, in_=source)
            else:
                nc.vector.tensor_copy(out=dealt, in_=source)
            g_codes = keep.tile([P, J], U32, name="g_codes%d" % a, align_bytes=64)
            g_plane = keep.tile([P, J], U8, name="g_plane%d" % a, align_bytes=64)
            nc.vector.quantize_mx(
                out=g_codes[:].bitcast(E5M2),
                scales=g_plane[:],
                in_=grouped[:].rearrange("p t m i -> p (t m i)"),
            )
            for t in range(PACK):
                cols = slice(P * t, P * (t + 1))
                nc.tensor.matmul_mx(
                    out=acc[t][:],
                    lhsT=g_codes[:, cols].bitcast(E5M2),
                    lhsT_scale=g_plane[:, cols],
                    rhs=w_codes[:, a, :].bitcast(E4M3),
                    rhs_scale=w_plane[:, a, :],
                    start=(a == 0),
                    stop=(a == PASSES - 1),
                )
        for t in range(PACK):
            nc.scalar.activation(out=scaled[t][:], in_=acc[t][:], func=COPY, scale=inv_col[:, t : t + 1])

        parts = keep.tile([P, PACK, BLOCKS], F32, name="parts")
        coef = keep.tile([P, PACK], F32, name="coef")
        spare = keep.tile([P, PACK, BLOCKS], F32, name="spare")

        def partial_sums(b, tag):
            product = keep.tile([P, PACK, P], F32, name="product%d" % b, tag=tag)
            for t in range(PACK):
                nc.vector.scalar_tensor_tensor(
                    out=product[:, t, :],
                    in0=xj[b // 2][t][:, (b % 2) * P : (b % 2 + 1) * P],
                    scalar=-1.0 / K,
                    in1=scaled[t][:, b * P : (b + 1) * P],
                    op0=MULT,
                    op1=MULT,
                    accum_out=parts[:, t, b : b + 1],
                )

        for n, b in enumerate(BLOCK_ORDER):
            x_picked = keep.tile([P, J], F32, name="x_picked%d" % b)
            nc.vector.tensor_copy(out=x_picked[:], in_=x_rows[b][:].indirect(offsets[:]))
            for t in range(PACK):
                nc.tensor.transpose(
                    xj[b // 2][t][:, (b % 2) * P : (b % 2 + 1) * P], x_picked[:, t::PACK], ident[:]
                )
            if n > 0:
                partial_sums(BLOCK_ORDER[n - 1], "x_rows%d" % b)
        partial_sums(BLOCK_ORDER[-1], "last_product")
        for t in range(PACK):
            nc.scalar.activation(out=spare[:, t, :], in_=parts[:, t, :], func=COPY, accum_out=coef[:, t : t + 1])

        y_codes = keep.tile([P, K], U32, name="y_codes", align_bytes=64)
        y_plane = keep.tile([P, K], U8, name="y_plane", align_bytes=64)
        out_rows = out_0.rearrange("(p t) k -> p t k", t=PACK)
        out_words = out_1[0].rearrange("p c r -> p (c r)").bitcast(I32)
        rounded = []
        for h in range(2):
            cols = slice(h * HALF, (h + 1) * HALF)
            y = keep.tile([P, PACK, HALF], F32, name="y%d" % h)
            for t in range(PACK):
                nc.vector.scalar_tensor_tensor(
                    out=y[:, t, :],
                    in0=xj[h][t],
                    scalar=coef[:, t : t + 1],
                    in1=scaled[t][:, cols],
                    op0=MULT,
                    op1=ADD,
                )
                if (t + 1) % (h + 1) == 0:
                    nc.sync.dma_start(out=out_rows[:, t - h : t + 1, cols], in_=y[:, t - h : t + 1, :])
            y_bf = keep.tile([P, HALF, PACK], BF16, name="y_bf%d" % h, align_bytes=64)
            source = y[:].rearrange("p t (c i) -> p c t i", i=PACK)
            woven = y_bf[:].rearrange("p (c i) t -> p c t i", i=PACK)
            if h == 0:
                nc.scalar.copy(out=woven, in_=source)
            else:
                nc.scalar.copy(out=woven[:, :SCALAR_RUNS], in_=source[:, :SCALAR_RUNS])
                nc.vector.tensor_copy(out=woven[:, SCALAR_RUNS:], in_=source[:, SCALAR_RUNS:])
            rounded.append(y_bf)
        for h in range(2):
            cols = slice(h * HALF, (h + 1) * HALF)
            nc.vector.quantize_mx(
                out=y_codes[:, cols].bitcast(E4M3),
                scales=y_plane[:, cols],
                in_=rounded[h][:].rearrange("p k t -> p (k t)"),
            )
            nc.sync.dma_start(out=out_words[:, cols], in_=y_codes[:, cols].bitcast(I32))
        for q in range(4):
            queue = nc.scalar if q < 2 else nc.sync
            queue.dma_start(
                out=out_2[0, 4 * q : 4 * q + 4, :].bitcast(I32),
                in_=y_plane[32 * q : 32 * q + 4, :].bitcast(I32),
            )
